import numpy as np
import ml_dtypes


def mxq(x, axis, fmt="e4m3"):
    dtype, down = {"e4m3": (ml_dtypes.float8_e4m3fn, 7), "e5m2": (ml_dtypes.float8_e5m2, 14)}[fmt]
    v = np.moveaxis(np.asarray(x, np.float32).astype(ml_dtypes.bfloat16).astype(np.float64), axis, -1)
    blocks = v.reshape(v.shape[:-1] + (-1, 32))
    amax = np.abs(blocks).max(-1, keepdims=True)
    byte = np.maximum(np.where(amax > 0, np.frexp(amax)[1] - 1 + 127, 0) - down, 1)
    scale = np.exp2(byte - 127.0)
    codes = (blocks / scale).astype(np.float32).astype(dtype).astype(np.float64)
    return np.moveaxis((codes * scale).reshape(v.shape), -1, axis)


WIDE = False


def mx_kscale(k):
    if not WIDE:
        return np.ones(k)
    levels = np.array([10, -10, 5, -5, 0])
    if k % 512:
        return np.exp2(np.random.permutation(np.resize(levels, k // 32))).repeat(32)
    a = np.empty((k // 512, 16))
    for p in range(k // 512):
        a[p, :8] = np.random.permutation(np.resize(levels, 8))
        for g in range(8):
            far = levels[np.abs(levels - a[p, g]) >= 10]
            a[p, g + 8] = far[np.random.randint(len(far))]
    return np.exp2(a.ravel()).repeat(32)


def f64(x):
    return np.asarray(x).astype(np.float64)


def striped(idx):
    return np.tile(idx.reshape(-1, 16).T, (8, 1)).astype(np.uint16)


def unstriped(offs):
    return offs[:16].T.reshape(-1).astype(np.int64)


def striped8(idx):
    return np.concatenate([x.reshape(-1, 16).T for x in idx]).astype(np.uint16)


def runs(offs, k):
    lists = np.stack([offs[16 * r : 16 * r + 16].T.reshape(-1) for r in range(8)]).astype(np.int64)
    return lists[np.arange(k) % 512 // 64]


def pack_weight(w):
    k, n = w.shape
    w = f64(np.asarray(w, np.float32).astype(ml_dtypes.bfloat16)).reshape(k // 32, 32, n)
    amax = np.abs(w).max(1)
    byte = np.clip(np.where(amax > 0, np.frexp(amax)[1] - 1 + 127 - 7, 1), 1, 254)
    scaled = (w * np.exp2(127.0 - byte)[:, None, :]).reshape(k, n).astype(np.float32)
    words = np.ascontiguousarray(scaled.reshape(k // 512, 128, 4, n).transpose(0, 1, 3, 2)).astype(ml_dtypes.float8_e4m3fn).view(np.uint8)
    return words, np.ascontiguousarray(byte.astype(np.uint8).reshape(k // 512, 16, n))


def unpack_weight(words, scales):
    g, p, n, _ = words.shape
    vals = np.ascontiguousarray(words).view(ml_dtypes.float8_e4m3fn).astype(np.float64) * np.repeat(np.exp2(scales.astype(np.float64) - 127.0), 8, axis=1)[..., None]
    return vals.transpose(0, 1, 3, 2).reshape(g * 512, n)


def sigmoid(v):
    return 1.0 / (1.0 + np.exp(-np.maximum(v, -700.0)))


K, T, S, H, W, G = 512, 1024, 256, 512, 192, 2048


def setup_inputs():
    n = np.random.standard_normal
    s = mx_kscale(K)[:, None]
    packed_xT = pack_weight(n((K, T)) * s)
    packed_w1 = pack_weight(n((K, H)) / np.sqrt(2 * K) / s)
    packed_w2 = pack_weight(n((K, H)) / np.sqrt(2 * K) / s)
    packed_dT = pack_weight(n((K, G)) / s)
    return {
        "x_words": packed_xT[0],
        "x_scales": packed_xT[1],
        "w1_words": packed_w1[0],
        "w1_scales": packed_w1[1],
        "w2_words": packed_w2[0],
        "w2_scales": packed_w2[1],
        "gs": (np.random.uniform(0.5, 1.5, (K, 1)) * s).astype(np.float32),
        "d_words": packed_dT[0],
        "d_scales": packed_dT[1],
        "sl": np.random.uniform(1.0, 2.0, (H, 1)).astype(np.float32),
        "th": (0.5 * n((H, 1))).astype(np.float32),
        "offs": striped(np.random.permutation(T)[:S]),
        "hz": striped8(np.random.randint(0, T, (8, S))),
        "n1": striped(np.random.permutation(S)[:W]),
        "n2": striped(np.random.permutation(S)[:W]),
        "k1": striped8(np.random.randint(0, G, (8, H))),
        "n3": striped8(np.stack([np.random.permutation(S) for _ in range(8)])),
        "n4": striped8(np.stack([np.random.permutation(S) for _ in range(8)])),
    }


def reference(x_words, x_scales, w1_words, w1_scales, w2_words, w2_scales, gs, d_words, d_scales, sl, th, offs, hz, n1, n2, k1, n3, n4):
    d_k1 = unpack_weight(d_words, d_scales)[np.arange(K)[:, None], runs(k1, K)]
    xq = unpack_weight(x_words, x_scales)[:, unstriped(offs)]
    x_hz = unpack_weight(x_words, x_scales)[np.arange(K)[:, None], runs(hz, K)]
    y = unpack_weight(w1_words, w1_scales).T @ xq + unpack_weight(w2_words, w2_scales).T @ x_hz
    old = y[:, unstriped(n1)]
    pa = y[:, unstriped(n2)]
    ra = old - (0.5 * pa)
    ds = y.copy()
    ds[:, unstriped(n1)] = ra
    z = f64(gs) * ds
    h = 0.0625 * ((d_k1.T @ mxq(z, 0, "e4m3")))
    sg = sigmoid(f64(sl) * (h[np.arange(H)[:, None], runs(n3, H)] - f64(th)))
    return (h[np.arange(H)[:, None], runs(n4, H)]) * sg

@@ -1,0 +1,197 @@
+from contextlib import ExitStack
+
+import concourse.mybir as mybir
+
+F32 = mybir.dt.float32
+BF16 = mybir.dt.bfloat16
+I32 = mybir.dt.int32
+U32 = mybir.dt.uint32
+U16 = mybir.dt.uint16
+U8 = mybir.dt.uint8
+FP8X4 = mybir.dt.float8_e4m3fn_x4
+ACT = mybir.ActivationFunctionType
+ALU = mybir.AluOpType
+
+P = 128
+PACK = 4
+K, T, S, H, W, G = 512, 1024, 256, 512, 192, 2048
+HALF = S // 2
+FLOPS = 3 * 2 * K * H * S
+
+
+def words_of(dram):
+    return dram[0].rearrange("p c r -> p (c r)").bitcast(I32)
+
+
+def spread_scales(dram):
+    rows = dram[0].bitcast(I32)
+    return rows.unsqueeze(1).to_broadcast([16, 8, rows.shape[1]])
+
+
+def place_rows(queue, dst, src):
+    for s in (1, 2, 3):
+        queue.dma_start(dst[s:P:32, :].bitcast(I32), src[8 * s:P:32, :].bitcast(I32))
+
+
+def tile_picked_thqkdifemg_none_p_kernel(
+    tc, x_words, x_scales, w1_words, w1_scales, w2_words, w2_scales, gs, d_words, d_scales,
+    sl, th, offs, hz, n1, n2, k1, n3, n4, out,
+):
+    nc = tc.nc
+    with ExitStack() as ctx:
+        sb = ctx.enter_context(tc.tile_pool(name="sb", bufs=1))
+        ps = ctx.enter_context(tc.psum_pool(name="ps", bufs=1))
+
+        def tile(name, shape, dtype, tag=None):
+            return sb.tile(shape, dtype, name=name, tag=tag or name, align_bytes=64)
+
+        def load_list(name, dram):
+            held = tile(name, list(dram.shape), U16)
+            nc.sync.dma_start(held[:], dram)
+            return held
+
+        h_win = [tile("h_win%d" % t, [P, 2 * S], F32) for t in range(PACK)]
+        for t in range(PACK):
+            nc.vector.memset(h_win[t][:, S:], 0.0)
+
+        hz_l = load_list("hz_l", hz)
+        xs_win = tile("xs_win", [P, T], U8)
+        nc.scalar.dma_start(xs_win[:].bitcast(I32), spread_scales(x_scales))
+        offs_l = load_list("offs_l", offs)
+        ws_raw = tile("ws_raw", [P, 2 * H], U8)
+        for a, sc in enumerate((w1_scales, w2_scales)):
+            nc.scalar.dma_start(ws_raw[:, a * H:(a + 1) * H].bitcast(I32), spread_scales(sc))
+        xw_win = tile("xw_win", [P, T], U32)
+        nc.sync.dma_start(xw_win[:].bitcast(I32), words_of(x_words))
+        n1_l = load_list("n1_l", n1)
+        n2_l = load_list("n2_l", n2)
+        ww_raw = [tile("ww_raw%d" % a, [P, H], U32) for a in range(2)]
+        for a, wd in enumerate((w1_words, w2_words)):
+            nc.sync.dma_start(ww_raw[a][:].bitcast(I32), words_of(wd))
+        ws_pl = tile("ws_pl", [P, 2 * H], U8)
+        nc.scalar.copy(ws_pl[:].bitcast(U32), ws_raw[:].bitcast(U32))
+        place_rows(nc.scalar, ws_pl, ws_raw)
+
+        xs_g = tile("xs_g", [P, 2 * S], U8)
+        nc.vector.tensor_copy(xs_g[:, S:], xs_win[:].indirect(hz_l[:]))
+        nc.vector.tensor_copy(xs_g[:, :S], xs_win[:].indirect(offs_l[:]))
+        xs = tile("xs", [P, 2 * S], U8)
+        nc.vector.tensor_copy(xs[:].bitcast(I32), xs_g[:].bitcast(I32))
+        place_rows(nc.sync, xs, xs_g)
+        ow_g = tile("ow_g", [P, S], U32)
+        nc.vector.tensor_copy(ow_g[:], xw_win[:].indirect(offs_l[:]))
+        hw_g = tile("hw_g", [P, S], U32)
+        nc.vector.tensor_copy(hw_g[:], xw_win[:].indirect(hz_l[:]))
+
+        ww = [tile("ww%d" % a, [P, H], U32) for a in range(2)]
+        ws = [tile("ws%d" % t, [P, 2 * P], U8) for t in range(PACK)]
+        for a in range(2):
+            nc.scalar.copy(ww[a][:].rearrange("p (t m) -> p m t", t=PACK),
+                           ww_raw[a][:].rearrange("p (m t) -> p m t", t=PACK))
+        for t in range(PACK):
+            nc.vector.tensor_copy(ws[t][:], ws_pl[:, t::PACK])
+
+        ds_win = tile("ds_win", [P, G], U8)
+        nc.sync.dma_start(ds_win[:].bitcast(I32), spread_scales(d_scales))
+        k1_l = load_list("k1_l", k1)
+        dw_win = tile("dw_win", [P, G], U32)
+        nc.sync.dma_start(dw_win[:].bitcast(I32), words_of(d_words))
+        gs_t = tile("gs_t", [P, PACK], F32)
+        sl_t = tile("sl_t", [P, PACK], F32)
+        th_t = tile("th_t", [P, PACK], F32)
+        for held, dram in ((gs_t, gs), (sl_t, sl), (th_t, th)):
+            nc.gpsimd.dma_start(held[:], dram.rearrange("(p t) o -> p (t o)", t=PACK))
+        n3_l = load_list("n3_l", n3)
+        n4_l = load_list("n4_l", n4)
+
+        y = [tile("y%d" % t, [P, S], F32) for t in range(PACK)]
+        for t in range(PACK):
+            cols = slice(t * P, (t + 1) * P)
+            acc = ps.tile([P, S], F32, name="y_acc%d" % t)
+            nc.tensor.matmul_mx(acc[:], lhsT=ww[0][:, cols].bitcast(FP8X4), lhsT_scale=ws[t][:, :P],
+                                rhs=ow_g[:].bitcast(FP8X4), rhs_scale=xs[:, :S], start=True, stop=False)
+            nc.tensor.matmul_mx(acc[:], lhsT=ww[1][:, cols].bitcast(FP8X4), lhsT_scale=ws[t][:, P:],
+                                rhs=hw_g[:].bitcast(FP8X4), rhs_scale=xs[:, S:], start=False, stop=True)
+            nc.vector.tensor_copy(y[t][:], acc[:])
+
+        old = [tile("old%d" % t, [P, W], F32) for t in range(PACK)]
+        pa = [tile("pa%d" % t, [P, W], F32) for t in range(PACK)]
+        ra = {}
+        ra_tag = {2: "after_code_scales", 3: "after_code_words0"}
+
+        def fetch(t):
+            nc.scalar.activation(old[t][:], y[t][:].indirect(n1_l[:]), ACT.Copy)
+            nc.scalar.activation(pa[t][:], y[t][:].indirect(n2_l[:]), ACT.Copy)
+            ra.setdefault(t, tile("ra%d" % t, [P, W], F32, ra_tag.get(t)))
+            nc.vector.scalar_tensor_tensor(ra[t][:], pa[t][:], -0.5, old[t][:], ALU.mult, ALU.add)
+
+        def put(t):
+            nc.scalar.activation(y[t][:].indirect(n1_l[:]), ra[t][:], ACT.Copy)
+
+        ds_d = tile("ds_d", [P, H], U8)
+        ds_p = tile("ds_p", [P, H], U8)
+        dw = tile("dw", [P, H], U32)
+
+        def code_scales():
+            ds_g = tile("ds_g", [P, H], U8, "after_code_scales")
+            for u in range(2):
+                nc.vector.tensor_copy(ds_g[:, u * 256:(u + 1) * 256], ds_win[:].indirect(k1_l[:, u * 16:(u + 1) * 16]))
+            nc.vector.tensor_copy(ds_d[:].rearrange("p (t m) -> p t m", t=PACK),
+                                  ds_g[:].rearrange("p (m t) -> p t m", t=PACK))
+            nc.vector.tensor_copy(ds_p[:].bitcast(I32), ds_d[:].bitcast(I32))
+            place_rows(nc.sync, ds_p, ds_d)
+
+        def code_words():
+            dealt = dw[:].rearrange("p (t u m) -> p u m t", t=PACK, u=2)
+            dw_g = [tile("dw_g%d" % u, [P, H // 2], U32, "after_code_words%d" % u) for u in range(2)]
+            for u in range(2):
+                nc.vector.tensor_copy(dw_g[u][:], dw_win[:].indirect(k1_l[:, u * 16:(u + 1) * 16]))
+            for u in range(2):
+                nc.vector.tensor_copy(dealt[:, u], dw_g[u][:].rearrange("p (m t) -> p m t", t=PACK))
+
+        bias = tile("bias", [P, PACK], F32)
+
+        fetch(0)
+        fetch(1)
+        put(0)
+        code_scales()
+        fetch(2)
+        put(1)
+        code_words()
+        fetch(3)
+        put(2)
+        put(3)
+        nc.vector.scalar_tensor_tensor(bias[:], sl_t[:], -1.0, th_t[:], ALU.mult, ALU.mult)
+
+        z = tile("z", [P, S, PACK], BF16, "after_code_words1")
+        zw = tile("zw", [P, S], U32)
+        zs = tile("zs", [P, S], U8)
+        halves = [slice(u * HALF, (u + 1) * HALF) for u in range(2)]
+        for t in range(PACK - 1):
+            nc.vector.tensor_scalar(z[:, :, t], y[t][:], gs_t[:, t:t + 1], None, ALU.mult)
+        last = PACK - 1
+        for cols in halves:
+            nc.vector.tensor_scalar(z[:, cols, last], y[last][:, cols], gs_t[:, last:], None, ALU.mult)
+        for cols in halves:
+            nc.vector.quantize_mx(out=zw[:, cols].bitcast(FP8X4), scales=zs[:, cols],
+                                  in_=z[:, cols, :].rearrange("p c t -> p (c t)"))
+
+        out_rows = out.rearrange("(p t) j -> p t j", t=PACK)
+        for t in range(PACK):
+            rows = slice(t * P, (t + 1) * P)
+            acc = ps.tile([P, S], F32, name="h_acc%d" % t)
+            for cols in (halves if t == 0 else [slice(0, S)]):
+                nc.tensor.matmul_mx(acc[:, cols], lhsT=dw[:, rows].bitcast(FP8X4), lhsT_scale=ds_p[:, rows],
+                                    rhs=zw[:, cols].bitcast(FP8X4), rhs_scale=zs[:, cols], start=True, stop=True)
+            nc.vector.tensor_scalar(h_win[t][:, :S], acc[:], 0.0625, None, ALU.mult)
+        for t in range(PACK):
+            sg = tile("sg%d" % t, [P, S], F32)
+            nc.scalar.activation(sg[:], h_win[t][:].indirect(n3_l[:]), ACT.Sigmoid,
+                                 bias=bias[:, t:t + 1], scale=sl_t[:, t:t + 1])
+            for u, cols in enumerate(halves if t == last else [slice(0, S)]):
+                width = cols.stop - cols.start
+                hv = tile("hv%d_%d" % (t, u), [P, width], F32)
+                res = tile("res%d_%d" % (t, u), [P, width], F32)
+                nc.scalar.activation(hv[:], h_win[t][:].indirect(n4_l[:, cols.start // 16:cols.stop // 16]), ACT.Copy)
+                nc.vector.tensor_tensor(res[:], hv[:], sg[:, cols], ALU.mult)
+                nc.sync.dma_start(out_rows[:, t, cols], res[:])

@@ -53,6 +53,10 @@ def tile_picked_thqkdifemg_none_p_kernel(
         h_win = [tile("h_win%d" % t, [P, 2 * S], F32) for t in range(PACK)]
         for t in range(PACK):
             nc.vector.memset(h_win[t][:, S:], 0.0)
+        warm_in = tile("warm_in", [P, 1], F32)
+        warm_out = tile("warm_out", [P, 1], F32)
+        nc.vector.memset(warm_in[:], 0.0)
+        nc.scalar.activation(warm_out[:], warm_in[:], ACT.Sigmoid)
 
         hz_l = load_list("hz_l", hz)
         xs_win = tile("xs_win", [P, T], U8)

@@ -50,13 +50,12 @@ def tile_picked_thqkdifemg_none_p_kernel(
             nc.sync.dma_start(held[:], dram)
             return held
 
-        h_win = [tile("h_win%d" % t, [P, 2 * S], F32) for t in range(PACK)]
-        for t in range(PACK):
-            nc.vector.memset(h_win[t][:, S:], 0.0)
         warm_in = tile("warm_in", [P, 1], F32)
         warm_out = tile("warm_out", [P, 1], F32)
         nc.vector.memset(warm_in[:], 0.0)
-        nc.scalar.activation(warm_out[:], warm_in[:], ACT.Sigmoid)
+        h_win = [tile("h_win%d" % t, [P, 2 * S], F32) for t in range(PACK)]
+        for t in range(PACK):
+            nc.vector.memset(h_win[t][:, S:], 0.0)
 
         hz_l = load_list("hz_l", hz)
         xs_win = tile("xs_win", [P, T], U8)
@@ -65,10 +64,10 @@ def tile_picked_thqkdifemg_none_p_kernel(
         ws_raw = tile("ws_raw", [P, 2 * H], U8)
         for a, sc in enumerate((w1_scales, w2_scales)):
             nc.scalar.dma_start(ws_raw[:, a * H:(a + 1) * H].bitcast(I32), spread_scales(sc))
+        nc.scalar.activation(warm_out[:], warm_in[:], ACT.Sigmoid)
+        n1_l = load_list("n1_l", n1)
         xw_win = tile("xw_win", [P, T], U32)
         nc.sync.dma_start(xw_win[:].bitcast(I32), words_of(x_words))
-        n1_l = load_list("n1_l", n1)
-        n2_l = load_list("n2_l", n2)
         ww_raw = [tile("ww_raw%d" % a, [P, H], U32) for a in range(2)]
         for a, wd in enumerate((w1_words, w2_words)):
             nc.sync.dma_start(ww_raw[a][:].bitcast(I32), words_of(wd))
@@ -82,6 +81,7 @@ def tile_picked_thqkdifemg_none_p_kernel(
         xs = tile("xs", [P, 2 * S], U8)
         nc.vector.tensor_copy(xs[:].bitcast(I32), xs_g[:].bitcast(I32))
         place_rows(nc.sync, xs, xs_g)
+        n2_l = load_list("n2_l", n2)
         ow_g = tile("ow_g", [P, S], U32)
         nc.vector.tensor_copy(ow_g[:], xw_win[:].indirect(offs_l[:]))
         hw_g = tile("hw_g", [P, S], U32)
@@ -89,9 +89,10 @@ def tile_picked_thqkdifemg_none_p_kernel(
 
         ww = [tile("ww%d" % a, [P, H], U32) for a in range(2)]
         ws = [tile("ws%d" % t, [P, 2 * P], U8) for t in range(PACK)]
-        for a in range(2):
-            nc.scalar.copy(ww[a][:].rearrange("p (t m) -> p m t", t=PACK),
-                           ww_raw[a][:].rearrange("p (m t) -> p m t", t=PACK))
+        for a, parts in enumerate(([slice(0, PACK)], [slice(0, 1), slice(1, PACK)])):
+            for part in parts:
+                nc.scalar.copy(ww[a][:].rearrange("p (t m) -> p m t", t=PACK)[:, :, part],
+                               ww_raw[a][:].rearrange("p (m t) -> p m t", t=PACK)[:, :, part])
         for t in range(PACK):
             nc.vector.tensor_copy(ws[t][:], ws_pl[:, t::PACK])
 
@@ -104,19 +105,22 @@ def tile_picked_thqkdifemg_none_p_kernel(
         sl_t = tile("sl_t", [P, PACK], F32)
         th_t = tile("th_t", [P, PACK], F32)
         for held, dram in ((gs_t, gs), (sl_t, sl), (th_t, th)):
-            nc.gpsimd.dma_start(held[:], dram.rearrange("(p t) o -> p (t o)", t=PACK))
+            nc.sync.dma_start(held[:], dram.rearrange("(p t) o -> p (t o)", t=PACK))
         n3_l = load_list("n3_l", n3)
         n4_l = load_list("n4_l", n4)
 
         y = [tile("y%d" % t, [P, S], F32) for t in range(PACK)]
+        halves = [slice(u * HALF, (u + 1) * HALF) for u in range(2)]
+        whole = [slice(0, S)]
         for t in range(PACK):
-            cols = slice(t * P, (t + 1) * P)
-            acc = ps.tile([P, S], F32, name="y_acc%d" % t)
-            nc.tensor.matmul_mx(acc[:], lhsT=ww[0][:, cols].bitcast(FP8X4), lhsT_scale=ws[t][:, :P],
-                                rhs=ow_g[:].bitcast(FP8X4), rhs_scale=xs[:, :S], start=True, stop=False)
-            nc.tensor.matmul_mx(acc[:], lhsT=ww[1][:, cols].bitcast(FP8X4), lhsT_scale=ws[t][:, P:],
-                                rhs=hw_g[:].bitcast(FP8X4), rhs_scale=xs[:, S:], start=False, stop=True)
-            nc.vector.tensor_copy(y[t][:], acc[:])
+            rows = slice(t * P, (t + 1) * P)
+            for u, cols in enumerate(halves if t == 0 else whole):
+                acc = ps.tile([P, cols.stop - cols.start], F32, name="y_acc%d_%d" % (t, u), tag="bank%d_%d" % (t, u))
+                nc.tensor.matmul_mx(acc[:], lhsT=ww[0][:, rows].bitcast(FP8X4), lhsT_scale=ws[t][:, :P],
+                                    rhs=ow_g[:, cols].bitcast(FP8X4), rhs_scale=xs[:, :S][:, cols], start=True, stop=False)
+                nc.tensor.matmul_mx(acc[:], lhsT=ww[1][:, rows].bitcast(FP8X4), lhsT_scale=ws[t][:, P:],
+                                    rhs=hw_g[:, cols].bitcast(FP8X4), rhs_scale=xs[:, S:][:, cols], start=False, stop=True)
+                nc.vector.tensor_copy(y[t][:, cols], acc[:])
 
         old = [tile("old%d" % t, [P, W], F32) for t in range(PACK)]
         pa = [tile("pa%d" % t, [P, W], F32) for t in range(PACK)]
@@ -170,7 +174,6 @@ def tile_picked_thqkdifemg_none_p_kernel(
         z = tile("z", [P, S, PACK], BF16, "after_code_words1")
         zw = tile("zw", [P, S], U32)
         zs = tile("zs", [P, S], U8)
-        halves = [slice(u * HALF, (u + 1) * HALF) for u in range(2)]
         for t in range(PACK - 1):
             nc.vector.tensor_scalar(z[:, :, t], y[t][:], gs_t[:, t:t + 1], None, ALU.mult)
         last = PACK - 1
@@ -183,19 +186,20 @@ def tile_picked_thqkdifemg_none_p_kernel(
         out_rows = out.rearrange("(p t) j -> p t j", t=PACK)
         for t in range(PACK):
             rows = slice(t * P, (t + 1) * P)
-            acc = ps.tile([P, S], F32, name="h_acc%d" % t)
-            for cols in (halves if t == 0 else [slice(0, S)]):
-                nc.tensor.matmul_mx(acc[:, cols], lhsT=dw[:, rows].bitcast(FP8X4), lhsT_scale=ds_p[:, rows],
+            for u, cols in enumerate(halves if t == 0 else whole):
+                acc = ps.tile([P, cols.stop - cols.start], F32, name="h_acc%d_%d" % (t, u), tag="bank%d_%d" % (t, u))
+                nc.tensor.matmul_mx(acc[:], lhsT=dw[:, rows].bitcast(FP8X4), lhsT_scale=ds_p[:, rows],
                                     rhs=zw[:, cols].bitcast(FP8X4), rhs_scale=zs[:, cols], start=True, stop=True)
-            nc.vector.tensor_scalar(h_win[t][:, :S], acc[:], 0.0625, None, ALU.mult)
+                nc.vector.tensor_scalar(h_win[t][:, cols], acc[:], 0.0625, None, ALU.mult)
         for t in range(PACK):
             sg = tile("sg%d" % t, [P, S], F32)
             nc.scalar.activation(sg[:], h_win[t][:].indirect(n3_l[:]), ACT.Sigmoid,
                                  bias=bias[:, t:t + 1], scale=sl_t[:, t:t + 1])
-            for u, cols in enumerate(halves if t == last else [slice(0, S)]):
+            for u, cols in enumerate([slice(0, S - 64), slice(S - 64, S)] if t == last else whole):
                 width = cols.stop - cols.start
                 hv = tile("hv%d_%d" % (t, u), [P, width], F32)
                 res = tile("res%d_%d" % (t, u), [P, width], F32)
-                nc.scalar.activation(hv[:], h_win[t][:].indirect(n4_l[:, cols.start // 16:cols.stop // 16]), ACT.Copy)
+                window = h_win[t][:, :S] if width == 64 else h_win[t][:]
+                nc.scalar.activation(hv[:], window.indirect(n4_l[:, cols.start // 16:cols.stop // 16]), ACT.Copy)
                 nc.vector.tensor_tensor(res[:], hv[:], sg[:, cols], ALU.mult)
                 nc.sync.dma_start(out_rows[:, t, cols], res[:])

from contextlib import ExitStack

import concourse.mybir as mybir

F32 = mybir.dt.float32
BF16 = mybir.dt.bfloat16
I32 = mybir.dt.int32
U32 = mybir.dt.uint32
U16 = mybir.dt.uint16
U8 = mybir.dt.uint8
FP8X4 = mybir.dt.float8_e4m3fn_x4
ACT = mybir.ActivationFunctionType
ALU = mybir.AluOpType

P = 128
PACK = 4
K, T, S, H, W, G = 512, 1024, 256, 512, 192, 2048
HALF = S // 2
FLOPS = 3 * 2 * K * H * S


def words_of(dram):
    return dram[0].rearrange("p c r -> p (c r)").bitcast(I32)


def spread_scales(dram):
    rows = dram[0].bitcast(I32)
    return rows.unsqueeze(1).to_broadcast([16, 8, rows.shape[1]])


def place_rows(queue, dst, src):
    for s in (1, 2, 3):
        queue.dma_start(dst[s:P:32, :].bitcast(I32), src[8 * s:P:32, :].bitcast(I32))


def tile_picked_thqkdifemg_none_p_kernel(
    tc, x_words, x_scales, w1_words, w1_scales, w2_words, w2_scales, gs, d_words, d_scales,
    sl, th, offs, hz, n1, n2, k1, n3, n4, out,
):
    nc = tc.nc
    with ExitStack() as ctx:
        sb = ctx.enter_context(tc.tile_pool(name="sb", bufs=1))
        ps = ctx.enter_context(tc.psum_pool(name="ps", bufs=1))

        def tile(name, shape, dtype, tag=None):
            return sb.tile(shape, dtype, name=name, tag=tag or name, align_bytes=64)

        def load_list(name, dram):
            held = tile(name, list(dram.shape), U16)
            nc.sync.dma_start(held[:], dram)
            return held

        warm_in = tile("warm_in", [P, 1], F32)
        warm_out = tile("warm_out", [P, 1], F32)
        nc.vector.memset(warm_in[:], 0.0)
        h_win = [tile("h_win%d" % t, [P, 2 * S], F32) for t in range(PACK)]
        for t in range(PACK):
            nc.vector.memset(h_win[t][:, S:], 0.0)

        hz_l = load_list("hz_l", hz)
        xs_win = tile("xs_win", [P, T], U8)
        nc.scalar.dma_start(xs_win[:].bitcast(I32), spread_scales(x_scales))
        offs_l = load_list("offs_l", offs)
        ws_raw = tile("ws_raw", [P, 2 * H], U8)
        for a, sc in enumerate((w1_scales, w2_scales)):
            nc.scalar.dma_start(ws_raw[:, a * H:(a + 1) * H].bitcast(I32), spread_scales(sc))
        nc.scalar.activation(warm_out[:], warm_in[:], ACT.Sigmoid)
        n1_l = load_list("n1_l", n1)
        xw_win = tile("xw_win", [P, T], U32)
        nc.sync.dma_start(xw_win[:].bitcast(I32), words_of(x_words))
        ww_raw = [tile("ww_raw%d" % a, [P, H], U32) for a in range(2)]
        for a, wd in enumerate((w1_words, w2_words)):
            nc.sync.dma_start(ww_raw[a][:].bitcast(I32), words_of(wd))
        ws_pl = tile("ws_pl", [P, 2 * H], U8)
        nc.scalar.copy(ws_pl[:].bitcast(U32), ws_raw[:].bitcast(U32))
        place_rows(nc.scalar, ws_pl, ws_raw)

        xs_g = tile("xs_g", [P, 2 * S], U8)
        nc.vector.tensor_copy(xs_g[:, S:], xs_win[:].indirect(hz_l[:]))
        nc.vector.tensor_copy(xs_g[:, :S], xs_win[:].indirect(offs_l[:]))
        xs = tile("xs", [P, 2 * S], U8)
        nc.vector.tensor_copy(xs[:].bitcast(I32), xs_g[:].bitcast(I32))
        place_rows(nc.sync, xs, xs_g)
        n2_l = load_list("n2_l", n2)
        ow_g = tile("ow_g", [P, S], U32)
        nc.vector.tensor_copy(ow_g[:], xw_win[:].indirect(offs_l[:]))
        hw_g = tile("hw_g", [P, S], U32)
        nc.vector.tensor_copy(hw_g[:], xw_win[:].indirect(hz_l[:]))

        ww = [tile("ww%d" % a, [P, H], U32) for a in range(2)]
        ws = [tile("ws%d" % t, [P, 2 * P], U8) for t in range(PACK)]
        for a, parts in enumerate(([slice(0, PACK)], [slice(0, 1), slice(1, PACK)])):
            for part in parts:
                nc.scalar.copy(ww[a][:].rearrange("p (t m) -> p m t", t=PACK)[:, :, part],
                               ww_raw[a][:].rearrange("p (m t) -> p m t", t=PACK)[:, :, part])
        for t in range(PACK):
            nc.vector.tensor_copy(ws[t][:], ws_pl[:, t::PACK])

        ds_win = tile("ds_win", [P, G], U8)
        nc.sync.dma_start(ds_win[:].bitcast(I32), spread_scales(d_scales))
        k1_l = load_list("k1_l", k1)
        dw_win = tile("dw_win", [P, G], U32)
        nc.sync.dma_start(dw_win[:].bitcast(I32), words_of(d_words))
        gs_t = tile("gs_t", [P, PACK], F32)
        sl_t = tile("sl_t", [P, PACK], F32)
        th_t = tile("th_t", [P, PACK], F32)
        for held, dram in ((gs_t, gs), (sl_t, sl), (th_t, th)):
            nc.sync.dma_start(held[:], dram.rearrange("(p t) o -> p (t o)", t=PACK))
        n3_l = load_list("n3_l", n3)
        n4_l = load_list("n4_l", n4)

        y = [tile("y%d" % t, [P, S], F32) for t in range(PACK)]
        halves = [slice(u * HALF, (u + 1) * HALF) for u in range(2)]
        whole = [slice(0, S)]
        for t in range(PACK):
            rows = slice(t * P, (t + 1) * P)
            for u, cols in enumerate(halves if t == 0 else whole):
                acc = ps.tile([P, cols.stop - cols.start], F32, name="y_acc%d_%d" % (t, u), tag="bank%d_%d" % (t, u))
                nc.tensor.matmul_mx(acc[:], lhsT=ww[0][:, rows].bitcast(FP8X4), lhsT_scale=ws[t][:, :P],
                                    rhs=ow_g[:, cols].bitcast(FP8X4), rhs_scale=xs[:, :S][:, cols], start=True, stop=False)
                nc.tensor.matmul_mx(acc[:], lhsT=ww[1][:, rows].bitcast(FP8X4), lhsT_scale=ws[t][:, P:],
                                    rhs=hw_g[:, cols].bitcast(FP8X4), rhs_scale=xs[:, S:][:, cols], start=False, stop=True)
                nc.vector.tensor_copy(y[t][:, cols], acc[:])

        old = [tile("old%d" % t, [P, W], F32) for t in range(PACK)]
        pa = [tile("pa%d" % t, [P, W], F32) for t in range(PACK)]
        ra = {}
        ra_tag = {2: "after_code_scales", 3: "after_code_words0"}

        def fetch(t):
            nc.scalar.activation(old[t][:], y[t][:].indirect(n1_l[:]), ACT.Copy)
            nc.scalar.activation(pa[t][:], y[t][:].indirect(n2_l[:]), ACT.Copy)
            ra.setdefault(t, tile("ra%d" % t, [P, W], F32, ra_tag.get(t)))
            nc.vector.scalar_tensor_tensor(ra[t][:], pa[t][:], -0.5, old[t][:], ALU.mult, ALU.add)

        def put(t):
            nc.scalar.activation(y[t][:].indirect(n1_l[:]), ra[t][:], ACT.Copy)

        ds_d = tile("ds_d", [P, H], U8)
        ds_p = tile("ds_p", [P, H], U8)
        dw = tile("dw", [P, H], U32)

        def code_scales():
            ds_g = tile("ds_g", [P, H], U8, "after_code_scales")
            for u in range(2):
                nc.vector.tensor_copy(ds_g[:, u * 256:(u + 1) * 256], ds_win[:].indirect(k1_l[:, u * 16:(u + 1) * 16]))
            nc.vector.tensor_copy(ds_d[:].rearrange("p (t m) -> p t m", t=PACK),
                                  ds_g[:].rearrange("p (m t) -> p t m", t=PACK))
            nc.vector.tensor_copy(ds_p[:].bitcast(I32), ds_d[:].bitcast(I32))
            place_rows(nc.sync, ds_p, ds_d)

        def code_words():
            dealt = dw[:].rearrange("p (t u m) -> p u m t", t=PACK, u=2)
            dw_g = [tile("dw_g%d" % u, [P, H // 2], U32, "after_code_words%d" % u) for u in range(2)]
            for u in range(2):
                nc.vector.tensor_copy(dw_g[u][:], dw_win[:].indirect(k1_l[:, u * 16:(u + 1) * 16]))
            for u in range(2):
                nc.vector.tensor_copy(dealt[:, u], dw_g[u][:].rearrange("p (m t) -> p m t", t=PACK))

        bias = tile("bias", [P, PACK], F32)

        fetch(0)
        fetch(1)
        put(0)
        code_scales()
        fetch(2)
        put(1)
        code_words()
        fetch(3)
        put(2)
        put(3)
        nc.vector.scalar_tensor_tensor(bias[:], sl_t[:], -1.0, th_t[:], ALU.mult, ALU.mult)

        z = tile("z", [P, S, PACK], BF16, "after_code_words1")
        zw = tile("zw", [P, S], U32)
        zs = tile("zs", [P, S], U8)
        for t in range(PACK - 1):
            nc.vector.tensor_scalar(z[:, :, t], y[t][:], gs_t[:, t:t + 1], None, ALU.mult)
        last = PACK - 1
        for cols in halves:
            nc.vector.tensor_scalar(z[:, cols, last], y[last][:, cols], gs_t[:, last:], None, ALU.mult)
        for cols in halves:
            nc.vector.quantize_mx(out=zw[:, cols].bitcast(FP8X4), scales=zs[:, cols],
                                  in_=z[:, cols, :].rearrange("p c t -> p (c t)"))

        out_rows = out.rearrange("(p t) j -> p t j", t=PACK)
        for t in range(PACK):
            rows = slice(t * P, (t + 1) * P)
            for u, cols in enumerate(halves if t == 0 else whole):
                acc = ps.tile([P, cols.stop - cols.start], F32, name="h_acc%d_%d" % (t, u), tag="bank%d_%d" % (t, u))
                nc.tensor.matmul_mx(acc[:], lhsT=dw[:, rows].bitcast(FP8X4), lhsT_scale=ds_p[:, rows],
                                    rhs=zw[:, cols].bitcast(FP8X4), rhs_scale=zs[:, cols], start=True, stop=True)
                nc.vector.tensor_scalar(h_win[t][:, cols], acc[:], 0.0625, None, ALU.mult)
        for t in range(PACK):
            sg = tile("sg%d" % t, [P, S], F32)
            nc.scalar.activation(sg[:], h_win[t][:].indirect(n3_l[:]), ACT.Sigmoid,
                                 bias=bias[:, t:t + 1], scale=sl_t[:, t:t + 1])
            for u, cols in enumerate([slice(0, S - 64), slice(S - 64, S)] if t == last else whole):
                width = cols.stop - cols.start
                hv = tile("hv%d_%d" % (t, u), [P, width], F32)
                res = tile("res%d_%d" % (t, u), [P, width], F32)
                window = h_win[t][:, :S] if width == 64 else h_win[t][:]
                nc.scalar.activation(hv[:], window.indirect(n4_l[:, cols.start // 16:cols.stop // 16]), ACT.Copy)
                nc.vector.tensor_tensor(res[:], hv[:], sg[:, cols], ALU.mult)
                nc.sync.dma_start(out_rows[:, t, cols], res[:])
